import numpy as np
import ml_dtypes


def mxq(x, axis, fmt="e4m3"):
    dtype, down = {"e4m3": (ml_dtypes.float8_e4m3fn, 7), "e5m2": (ml_dtypes.float8_e5m2, 14)}[fmt]
    v = np.moveaxis(np.asarray(x, np.float32).astype(ml_dtypes.bfloat16).astype(np.float64), axis, -1)
    blocks = v.reshape(v.shape[:-1] + (-1, 32))
    amax = np.abs(blocks).max(-1, keepdims=True)
    byte = np.maximum(np.where(amax > 0, np.frexp(amax)[1] - 1 + 127, 0) - down, 1)
    scale = np.exp2(byte - 127.0)
    codes = (blocks / scale).astype(np.float32).astype(dtype).astype(np.float64)
    return np.moveaxis((codes * scale).reshape(v.shape), -1, axis)


WIDE = False


def mx_kscale(k):
    if not WIDE:
        return np.ones(k)
    levels = np.array([10, -10, 5, -5, 0])
    if k % 512:
        return np.exp2(np.random.permutation(np.resize(levels, k // 32))).repeat(32)
    a = np.empty((k // 512, 16))
    for p in range(k // 512):
        a[p, :8] = np.random.permutation(np.resize(levels, 8))
        for g in range(8):
            far = levels[np.abs(levels - a[p, g]) >= 10]
            a[p, g + 8] = far[np.random.randint(len(far))]
    return np.exp2(a.ravel()).repeat(32)


def f64(x):
    return np.asarray(x).astype(np.float64)


def striped(idx):
    return np.tile(np.asarray(idx).reshape(-1, 16).T, (8, 1)).astype(np.uint16)


def unstriped(offs):
    return offs[:16].T.reshape(-1).astype(np.int64)


E2M1 = np.array([0.0, 0.5, 1.0, 1.5, 2.0, 3.0, 4.0, 6.0, -0.0, -0.5, -1.0, -1.5, -2.0, -3.0, -4.0, -6.0])


def pack_weight(w, fmt):
    k, n = w.shape
    w = f64(np.asarray(w, np.float32).astype(ml_dtypes.bfloat16)).reshape(k // 32, 32, n)
    amax = np.abs(w).max(1)
    if fmt == "e4m3":
        byte = np.frexp(amax)[1] - 1 + 127 - 7
    else:
        mant, ex = np.frexp(amax / 6.0)
        byte = np.where(mant > 0.5, ex, ex - 1) + 127
    byte = np.clip(np.where(amax > 0, byte, 1), 1, 254)
    scaled = (w * np.exp2(127.0 - byte)[:, None, :]).reshape(k, n).astype(np.float32)
    by_word = np.ascontiguousarray(scaled.reshape(k // 512, 128, 4, n).transpose(0, 1, 3, 2))
    if fmt == "e4m3":
        words = by_word.astype(ml_dtypes.float8_e4m3fn).view(np.uint8)
    else:
        c = by_word.astype(ml_dtypes.float4_e2m1fn).view(np.uint8) & 0xF
        words = (c[..., 0::2] | (c[..., 1::2] << 4)).reshape(k // 512, 128, 2 * n)
    return np.ascontiguousarray(words), np.ascontiguousarray(byte.astype(np.uint8).reshape(k // 512, 16, n))


def unpack_weight(words, scales, fmt):
    g, _, n = scales.shape
    words = np.ascontiguousarray(words).reshape(g, 128, n, -1)
    if fmt == "e4m3":
        vals = words.view(ml_dtypes.float8_e4m3fn).astype(np.float64)
    else:
        nib = np.empty((g, 128, n, 4), np.uint8)
        nib[..., 0::2] = words & 0xF
        nib[..., 1::2] = words >> 4
        vals = E2M1[nib]
    vals = vals * np.repeat(np.exp2(scales.astype(np.float64) - 127.0), 8, axis=1)[..., None]
    return vals.transpose(0, 1, 3, 2).reshape(g * 512, n)


D, T, I, Q = 1024, 4096, 1024, 128


def setup_inputs():
    n = np.random.standard_normal
    idx = np.random.permutation(T)[:I]
    fd = mx_kscale(D)
    vocp = pack_weight(n((D, T)) / fd[:, None], "e2m1")
    return {
        "ha": (n((D, Q)) * 1.0 / np.sqrt(D) * fd[:, None]).astype(np.float32),
        "hb": (n((D, Q)) * 1.0 / np.sqrt(D) * fd[:, None]).astype(np.float32),
        "hc": (n((D, Q)) * 1.0 / np.sqrt(D) * fd[:, None]).astype(np.float32),
        "voc_words": vocp[0],
        "voc_scales": vocp[1],
        "pia": (np.random.uniform(0.2, 0.4, (Q, 1))).astype(np.float32),
        "pib": (np.random.uniform(0.2, 0.4, (Q, 1))).astype(np.float32),
        "pic": (np.random.uniform(0.2, 0.4, (Q, 1))).astype(np.float32),
        "offs": striped(idx),
    }


def reference(ha, hb, hc, voc_words, voc_scales, pia, pib, pic, offs):
    idx = unstriped(offs)
    vocu = unpack_weight(voc_words, voc_scales, "e2m1")
    haq = mxq(f64(ha), 0, "e4m3")
    vocidxg = vocu[:, idx]
    a = haq.T @ vocidxg
    hbq = mxq(f64(hb), 0, "e4m3")
    b = hbq.T @ vocidxg
    hcq = mxq(f64(hc), 0, "e4m3")
    r = hcq.T @ vocidxg
    pa = np.exp(a - np.max(a, axis=1, keepdims=True))
    pb = np.exp(b - np.max(b, axis=1, keepdims=True))
    pc = np.exp(r - np.max(r, axis=1, keepdims=True))
    y = (f64(pia) * pa / np.sum(pa, axis=1, keepdims=True) + f64(pib) * pb / np.sum(pb, axis=1, keepdims=True) + f64(pic) * pc / np.sum(pc, axis=1, keepdims=True)) * 512.0
    return y

@@ -1,0 +1,174 @@
+from contextlib import ExitStack
+
+import concourse.mybir as mybir
+
+F32 = mybir.dt.float32
+BF16 = mybir.dt.bfloat16
+I32 = mybir.dt.int32
+U32 = mybir.dt.uint32
+U16 = mybir.dt.uint16
+U8 = mybir.dt.uint8
+FP8X4 = mybir.dt.float8_e4m3fn_x4
+FP4X4 = mybir.dt.float4_e2m1fn_x4
+ALU = mybir.AluOpType
+ACT = mybir.ActivationFunctionType
+AX = mybir.AxisListType
+
+D, T, I, Q = 1024, 4096, 1024, 128
+P = 128
+PACK = 4
+PASSES = D // (P * PACK)
+HALF = 512
+HALVES = I // HALF
+LIST_COLS = I // 16
+SCALE_ROWS = 16
+SCALE_BASE = P - PASSES * SCALE_ROWS
+OUT_SCALE = 512.0
+STORE = 256
+
+FLOPS = 3 * 2 * D * Q * I
+
+
+def tile_attend_mixsoftmax_kernel(tc, ha, hb, hc, voc_words, voc_scales, pia, pib, pic, offs, out):
+    nc = tc.nc
+    hidden = (ha, hb, hc)
+    shares = (pia, pib, pic)
+    with ExitStack() as ctx:
+        keep = ctx.enter_context(tc.tile_pool(name="keep", bufs=1))
+        stage = ctx.enter_context(tc.tile_pool(name="stage", bufs=1))
+        psum = ctx.enter_context(tc.psum_pool(name="psum", bufs=1))
+
+        offsets = keep.tile([P, LIST_COLS], U16, name="offsets")
+        nc.sync.dma_start(offsets[:], offs)
+
+        scale_win = keep.tile([P, T], U8, name="scale_win", align_bytes=64)
+        nc.sync.dma_start(
+            out=scale_win[SCALE_BASE:P, :].bitcast(I32),
+            in_=voc_scales.rearrange("z f t -> (z f) t").bitcast(I32),
+        )
+        nc.vector.memset(scale_win[0:SCALE_BASE, :].bitcast(I32), 0)
+
+        word_win = [keep.tile([P, T], U16, name="word_win%d" % z, align_bytes=64) for z in range(PASSES)]
+        raw_bytes = PASSES * PACK * Q * 4
+        raw_at = (raw_bytes // 2, 0, raw_bytes)
+        raw = [stage.tile([P, PASSES, PACK * Q], F32, name="raw%d" % j, offset=raw_at[j]) for j in range(3)]
+
+        def load_words(z):
+            nc.scalar.dma_start(out=word_win[z][:].bitcast(I32), in_=voc_words[z].bitcast(I32))
+
+        def load_hidden(j):
+            nc.scalar.dma_start(out=raw[j][:], in_=hidden[j].rearrange("(z p t) q -> p z (t q)", z=PASSES, t=PACK))
+
+        load_words(0)
+        load_hidden(0)
+        load_words(1)
+
+        warm = keep.tile([P, 1], F32, name="warm")
+        warm_out = keep.tile([P, 1], F32, name="warm_out")
+        nc.gpsimd.memset(warm[:], 0.0)
+        nc.scalar.activation(out=warm_out[:], in_=warm[:], func=ACT.Exp)
+
+        share = [keep.tile([P, 1], F32, name="share%d" % j) for j in range(3)]
+        for j in range(3):
+            nc.gpsimd.dma_start(out=share[j][:], in_=shares[j])
+
+        plane = [keep.tile([P, I], U8, name="plane%d" % z, align_bytes=64) for z in range(PASSES)]
+        for z in range(PASSES):
+            nc.vector.memset(plane[z][:].bitcast(I32), 0)
+
+        scale_g = keep.tile([P, I], U8, name="scale_g", align_bytes=64)
+        nc.vector.tensor_copy(out=scale_g[:], in_=scale_win[:].indirect(offsets[:]))
+        for z in range(PASSES):
+            for quad in range(4):
+                row = SCALE_BASE + SCALE_ROWS * z + 4 * quad
+                nc.sync.dma_start(
+                    out=plane[z][32 * quad : 32 * quad + 4, :].bitcast(I32),
+                    in_=scale_g[row : row + 4, :].bitcast(I32),
+                )
+
+        codes = [keep.tile([P, PASSES * Q], U32, name="codes%d" % j, align_bytes=64) for j in range(3)]
+        hscale = [keep.tile([P, PASSES * Q], U8, name="hscale%d" % j, align_bytes=64) for j in range(3)]
+        grouped = [keep.tile([P, PASSES * Q * PACK], BF16, name="grouped%d" % j, tag="hold%d" % j, align_bytes=64) for j in range(3)]
+
+        def cast(j):
+            for z in range(PASSES):
+                nc.scalar.copy(
+                    out=grouped[j][:, z * Q * PACK : (z + 1) * Q * PACK].rearrange("p (c i t) -> p c t i", i=4, t=PACK),
+                    in_=raw[j][:, z, :].rearrange("p (t c i) -> p c t i", i=4, t=PACK),
+                )
+
+        def quantise(j):
+            nc.vector.quantize_mx(out=codes[j][:].bitcast(FP8X4), scales=hscale[j][:], in_=grouped[j][:])
+
+        first = keep.tile([P, I], U16, name="first", align_bytes=64)
+        nc.vector.tensor_copy(out=first[:], in_=word_win[0][:].indirect(offsets[:]))
+        cast(0)
+        load_hidden(1)
+        load_hidden(2)
+        quantise(0)
+        second = [keep.tile([P, HALF], U16, name="second%d" % h, align_bytes=64) for h in range(HALVES)]
+        cols = LIST_COLS // HALVES
+        for h in range(HALVES):
+            nc.vector.tensor_copy(out=second[h][:], in_=word_win[1][:].indirect(offsets[:, h * cols : (h + 1) * cols]))
+        cast(1)
+        cast(2)
+
+        def words(z, h):
+            return first[:, h * HALF : (h + 1) * HALF] if z == 0 else second[h][:]
+
+        bank = [[psum.tile([P, HALF], F32, name="bank%d_%d" % (j, h)) for h in range(HALVES)] for j in range(3)]
+        quantise(1)
+        quantise(2)
+        for j in range(3):
+            for z in range(PASSES):
+                for h in range(HALVES):
+                    nc.tensor.matmul_mx(
+                        out=bank[j][h][:],
+                        lhsT=codes[j][:, z * Q : (z + 1) * Q].bitcast(FP8X4),
+                        lhsT_scale=hscale[j][:, z * Q : (z + 1) * Q],
+                        rhs=words(z, h).bitcast(FP4X4),
+                        rhs_scale=plane[z][:, h * HALF : (h + 1) * HALF],
+                        start=(z == 0),
+                        stop=(z == PASSES - 1),
+                    )
+
+        prob, low0, sums = [], [], []
+        for j in range(3):
+            if j == 0:
+                pr = stage.tile([P, I], F32, name="prob0", offset=raw_at[2])
+            else:
+                pr = keep.tile([P, I], F32, name="prob%d" % j)
+            l0 = keep.tile([P, 1], F32, name="low0_%d" % j, tag=("hold2" if j == 1 else "low0_%d" % j), align_bytes=64)
+            negated = keep.tile([P, HALF], F32, name="negated%d" % j, tag=("hold1" if j == 0 else "negated%d" % j), align_bytes=64)
+            low = keep.tile([P, 1], F32, name="low_%d" % j)
+            nc.vector.tensor_reduce(out=l0[:], in_=bank[j][0][:], axis=AX.X, op=ALU.max, negate=True)
+            nc.vector.tensor_scalar(
+                out=negated[:], in0=bank[j][1][:], scalar1=-1.0, scalar2=l0[:],
+                op0=ALU.mult, op1=ALU.min, accum_out=low[:],
+            )
+            sum0 = keep.tile([P, 1], F32, name="sum0_%d" % j)
+            sum1 = keep.tile([P, 1], F32, name="sum1_%d" % j)
+            nc.scalar.activation(out=pr[:, 0:HALF], in_=bank[j][0][:], func=ACT.Exp, bias=low[:], scale=1.0, accum_out=sum0[:])
+            nc.scalar.activation(out=pr[:, HALF:I], in_=negated[:], func=ACT.Exp, bias=low[:], scale=-1.0, accum_out=sum1[:])
+            prob.append(pr)
+            sums.append((sum0, sum1))
+
+        mix = None
+        for j in range(3):
+            total = keep.tile([P, 1], F32, name="total_%d" % j, tag=("hold2", "low0_2", "total_2")[j], align_bytes=64)
+            inv = keep.tile([P, 1], F32, name="inv_%d" % j)
+            cf = keep.tile([P, 1], F32, name="coef_%d" % j)
+            nc.vector.tensor_tensor(out=total[:], in0=sums[j][0][:], in1=sums[j][1][:], op=ALU.add)
+            nc.vector.reciprocal(out=inv[:], in_=total[:])
+            nc.vector.tensor_scalar(out=cf[:], in0=inv[:], scalar1=share[j][:], scalar2=OUT_SCALE, op0=ALU.mult, op1=ALU.mult)
+            new = keep.tile([P, I], F32, name="mix%d" % j)
+            if j == 0:
+                nc.vector.tensor_scalar(out=new[:], in0=prob[j][:], scalar1=cf[:], scalar2=None, op0=ALU.mult)
+            elif j == 1:
+                nc.vector.scalar_tensor_tensor(out=new[:], in0=prob[j][:], scalar=cf[:], in1=mix[:], op0=ALU.mult, op1=ALU.add)
+            else:
+                for c0 in range(0, I, STORE):
+                    cs = slice(c0, c0 + STORE)
+                    nc.vector.scalar_tensor_tensor(out=new[:, cs], in0=prob[j][:, cs], scalar=cf[:], in1=mix[:, cs], op0=ALU.mult, op1=ALU.add)
+                    nc.sync.dma_start(out=out[:, cs], in_=new[:, cs])
+            mix = new

@@ -42,7 +42,7 @@ def tile_attend_mixsoftmax_kernel(tc, ha, hb, hc, voc_words, voc_scales, pia, pi
         nc.sync.dma_start(offsets[:], offs)
 
         scale_win = keep.tile([P, T], U8, name="scale_win", align_bytes=64)
-        nc.sync.dma_start(
+        nc.scalar.dma_start(
             out=scale_win[SCALE_BASE:P, :].bitcast(I32),
             in_=voc_scales.rearrange("z f t -> (z f) t").bitcast(I32),
         )
@@ -50,7 +50,7 @@ def tile_attend_mixsoftmax_kernel(tc, ha, hb, hc, voc_words, voc_scales, pia, pi
 
         word_win = [keep.tile([P, T], U16, name="word_win%d" % z, align_bytes=64) for z in range(PASSES)]
         raw_bytes = PASSES * PACK * Q * 4
-        raw_at = (raw_bytes // 2, 0, raw_bytes)
+        raw_at = (64, raw_bytes + 128, 128)
         raw = [stage.tile([P, PASSES, PACK * Q], F32, name="raw%d" % j, offset=raw_at[j]) for j in range(3)]
 
         def load_words(z):
@@ -62,21 +62,16 @@ def tile_attend_mixsoftmax_kernel(tc, ha, hb, hc, voc_words, voc_scales, pia, pi
         load_words(0)
         load_hidden(0)
         load_words(1)
+        load_hidden(1)
 
         warm = keep.tile([P, 1], F32, name="warm")
-        warm_out = keep.tile([P, 1], F32, name="warm_out")
         nc.gpsimd.memset(warm[:], 0.0)
-        nc.scalar.activation(out=warm_out[:], in_=warm[:], func=ACT.Exp)
-
-        share = [keep.tile([P, 1], F32, name="share%d" % j) for j in range(3)]
-        for j in range(3):
-            nc.gpsimd.dma_start(out=share[j][:], in_=shares[j])
 
         plane = [keep.tile([P, I], U8, name="plane%d" % z, align_bytes=64) for z in range(PASSES)]
         for z in range(PASSES):
             nc.vector.memset(plane[z][:].bitcast(I32), 0)
 
-        scale_g = keep.tile([P, I], U8, name="scale_g", align_bytes=64)
+        scale_g = stage.tile([P, I], U8, name="scale_g", offset=2 * raw_bytes + 128)
         nc.vector.tensor_copy(out=scale_g[:], in_=scale_win[:].indirect(offsets[:]))
         for z in range(PASSES):
             for quad in range(4):
@@ -85,6 +80,10 @@ def tile_attend_mixsoftmax_kernel(tc, ha, hb, hc, voc_words, voc_scales, pia, pi
                     out=plane[z][32 * quad : 32 * quad + 4, :].bitcast(I32),
                     in_=scale_g[row : row + 4, :].bitcast(I32),
                 )
+
+        share = [stage.tile([P, 1], F32, name="share%d" % j, offset=2 * raw_bytes + 128 + 64 * j) for j in range(3)]
+        for j in range(3):
+            nc.sync.dma_start(out=share[j][:], in_=shares[j])
 
         codes = [keep.tile([P, PASSES * Q], U32, name="codes%d" % j, align_bytes=64) for j in range(3)]
         hscale = [keep.tile([P, PASSES * Q], U8, name="hscale%d" % j, align_bytes=64) for j in range(3)]
@@ -103,25 +102,26 @@ def tile_attend_mixsoftmax_kernel(tc, ha, hb, hc, voc_words, voc_scales, pia, pi
         first = keep.tile([P, I], U16, name="first", align_bytes=64)
         nc.vector.tensor_copy(out=first[:], in_=word_win[0][:].indirect(offsets[:]))
         cast(0)
-        load_hidden(1)
         load_hidden(2)
+        warm_out = stage.tile([P, 1], F32, name="warm_out", offset=64)
+        nc.scalar.activation(out=warm_out[:], in_=warm[:], func=ACT.Exp)
         quantise(0)
-        second = [keep.tile([P, HALF], U16, name="second%d" % h, align_bytes=64) for h in range(HALVES)]
+        second = keep.tile([P, I], U16, name="second", tag="hold0", align_bytes=64)
         cols = LIST_COLS // HALVES
         for h in range(HALVES):
-            nc.vector.tensor_copy(out=second[h][:], in_=word_win[1][:].indirect(offsets[:, h * cols : (h + 1) * cols]))
+            nc.vector.tensor_copy(out=second[:, h * HALF : (h + 1) * HALF], in_=word_win[1][:].indirect(offsets[:, h * cols : (h + 1) * cols]))
         cast(1)
         cast(2)
 
         def words(z, h):
-            return first[:, h * HALF : (h + 1) * HALF] if z == 0 else second[h][:]
+            return (first, second)[z][:, h * HALF : (h + 1) * HALF]
 
         bank = [[psum.tile([P, HALF], F32, name="bank%d_%d" % (j, h)) for h in range(HALVES)] for j in range(3)]
         quantise(1)
         quantise(2)
         for j in range(3):
-            for z in range(PASSES):
-                for h in range(HALVES):
+            for h in range(HALVES):
+                for z in range(PASSES):
                     nc.tensor.matmul_mx(
                         out=bank[j][h][:],
                         lhsT=codes[j][:, z * Q : (z + 1) * Q].bitcast(FP8X4),
@@ -132,43 +132,57 @@ def tile_attend_mixsoftmax_kernel(tc, ha, hb, hc, voc_words, voc_scales, pia, pi
                         stop=(z == PASSES - 1),
                     )
 
-        prob, low0, sums = [], [], []
-        for j in range(3):
-            if j == 0:
-                pr = stage.tile([P, I], F32, name="prob0", offset=raw_at[2])
-            else:
-                pr = keep.tile([P, I], F32, name="prob%d" % j)
-            l0 = keep.tile([P, 1], F32, name="low0_%d" % j, tag=("hold2" if j == 1 else "low0_%d" % j), align_bytes=64)
-            negated = keep.tile([P, HALF], F32, name="negated%d" % j, tag=("hold1" if j == 0 else "negated%d" % j), align_bytes=64)
-            low = keep.tile([P, 1], F32, name="low_%d" % j)
-            nc.vector.tensor_reduce(out=l0[:], in_=bank[j][0][:], axis=AX.X, op=ALU.max, negate=True)
+        prob = [stage.tile([P, I], F32, name="prob0", offset=raw_at[2])]
+        prob += [keep.tile([P, I], F32, name="prob%d" % j) for j in (1, 2)]
+        negated = [keep.tile([P, I], F32, name="negated%d" % j) for j in range(3)]
+        total = [keep.tile([P, 1], F32, name="total_%d" % j) for j in range(3)]
+        coef = [keep.tile([P, 1], F32, name="coef_%d" % j) for j in range(3)]
+        mix = [keep.tile([P, I], F32, name="mix%d" % j) for j in range(3)]
+        part, inv = {}, {}
+
+        def first_max(j):
+            part[j] = keep.tile([P, 1], F32, name="part%d" % j, tag=("part0", "hold2", "part2")[j], align_bytes=64)
             nc.vector.tensor_scalar(
-                out=negated[:], in0=bank[j][1][:], scalar1=-1.0, scalar2=l0[:],
+                out=negated[j][:, 0:HALF], in0=bank[j][0][:], scalar1=-1.0, scalar2=None,
+                op0=ALU.mult, op1=ALU.min, accum_out=part[j][:],
+            )
+
+        def second_max(j):
+            low = keep.tile([P, 1], F32, name="low%d" % j, tag=("hold1", "low1", "low2")[j], align_bytes=64)
+            nc.vector.tensor_scalar(
+                out=negated[j][:, HALF:I], in0=bank[j][1][:], scalar1=-1.0, scalar2=part[j][:],
                 op0=ALU.mult, op1=ALU.min, accum_out=low[:],
             )
-            sum0 = keep.tile([P, 1], F32, name="sum0_%d" % j)
-            sum1 = keep.tile([P, 1], F32, name="sum1_%d" % j)
-            nc.scalar.activation(out=pr[:, 0:HALF], in_=bank[j][0][:], func=ACT.Exp, bias=low[:], scale=1.0, accum_out=sum0[:])
-            nc.scalar.activation(out=pr[:, HALF:I], in_=negated[:], func=ACT.Exp, bias=low[:], scale=-1.0, accum_out=sum1[:])
-            prob.append(pr)
-            sums.append((sum0, sum1))
+            nc.scalar.activation(out=prob[j][:], in_=negated[j][:], func=ACT.Exp, bias=low[:], scale=-1.0, accum_out=total[j][:])
 
-        mix = None
-        for j in range(3):
-            total = keep.tile([P, 1], F32, name="total_%d" % j, tag=("hold2", "low0_2", "total_2")[j], align_bytes=64)
-            inv = keep.tile([P, 1], F32, name="inv_%d" % j)
-            cf = keep.tile([P, 1], F32, name="coef_%d" % j)
-            nc.vector.tensor_tensor(out=total[:], in0=sums[j][0][:], in1=sums[j][1][:], op=ALU.add)
-            nc.vector.reciprocal(out=inv[:], in_=total[:])
-            nc.vector.tensor_scalar(out=cf[:], in0=inv[:], scalar1=share[j][:], scalar2=OUT_SCALE, op0=ALU.mult, op1=ALU.mult)
-            new = keep.tile([P, I], F32, name="mix%d" % j)
-            if j == 0:
-                nc.vector.tensor_scalar(out=new[:], in0=prob[j][:], scalar1=cf[:], scalar2=None, op0=ALU.mult)
-            elif j == 1:
-                nc.vector.scalar_tensor_tensor(out=new[:], in0=prob[j][:], scalar=cf[:], in1=mix[:], op0=ALU.mult, op1=ALU.add)
-            else:
-                for c0 in range(0, I, STORE):
-                    cs = slice(c0, c0 + STORE)
-                    nc.vector.scalar_tensor_tensor(out=new[:, cs], in0=prob[j][:, cs], scalar=cf[:], in1=mix[:, cs], op0=ALU.mult, op1=ALU.add)
-                    nc.sync.dma_start(out=out[:, cs], in_=new[:, cs])
-            mix = new
+        def invert(j):
+            inv[j] = keep.tile([P, 1], F32, name="inv%d" % j, tag=("hold2", "part2", "inv2")[j], align_bytes=64)
+            nc.vector.reciprocal(out=inv[j][:], in_=total[j][:])
+
+        def weight(j):
+            nc.vector.tensor_scalar(out=coef[j][:], in0=inv[j][:], scalar1=share[j][:], scalar2=OUT_SCALE, op0=ALU.mult, op1=ALU.mult)
+
+        def add_term(j, c0, c1):
+            nc.vector.scalar_tensor_tensor(
+                out=mix[j][:, c0:c1], in0=prob[j][:, c0:c1], scalar=coef[j][:], in1=mix[j - 1][:, c0:c1],
+                op0=ALU.mult, op1=ALU.add,
+            )
+
+        first_max(0)
+        second_max(0)
+        first_max(1)
+        second_max(1)
+        invert(0)
+        first_max(2)
+        weight(0)
+        second_max(2)
+        invert(1)
+        nc.vector.tensor_scalar(out=mix[0][:], in0=prob[0][:], scalar1=coef[0][:], scalar2=None, op0=ALU.mult)
+        weight(1)
+        invert(2)
+        weight(2)
+        add_term(1, 0, HALF)
+        add_term(1, HALF, I)
+        for c0 in range(0, I, STORE):
+            add_term(2, c0, c0 + STORE)
+            nc.sync.dma_start(out=out[:, c0 : c0 + STORE], in_=mix[2][:, c0 : c0 + STORE])

@@ -36,42 +36,41 @@ def tile_attend_mixsoftmax_kernel(tc, ha, hb, hc, voc_words, voc_scales, pia, pi
     with ExitStack() as ctx:
         keep = ctx.enter_context(tc.tile_pool(name="keep", bufs=1))
         stage = ctx.enter_context(tc.tile_pool(name="stage", bufs=1))
+        late = ctx.enter_context(tc.tile_pool(name="late", bufs=1))
         psum = ctx.enter_context(tc.psum_pool(name="psum", bufs=1))
 
         offsets = keep.tile([P, LIST_COLS], U16, name="offsets")
         nc.sync.dma_start(offsets[:], offs)
 
-        scale_win = keep.tile([P, T], U8, name="scale_win", align_bytes=64)
+        scale_win = stage.tile([P, T], U8, name="scale_win", offset=3840)
         nc.scalar.dma_start(
             out=scale_win[SCALE_BASE:P, :].bitcast(I32),
             in_=voc_scales.rearrange("z f t -> (z f) t").bitcast(I32),
         )
         nc.vector.memset(scale_win[0:SCALE_BASE, :].bitcast(I32), 0)
 
-        word_win = [keep.tile([P, T], U16, name="word_win%d" % z, align_bytes=64) for z in range(PASSES)]
-        raw_bytes = PASSES * PACK * Q * 4
-        raw_at = (64, raw_bytes + 128, 128)
-        raw = [stage.tile([P, PASSES, PACK * Q], F32, name="raw%d" % j, offset=raw_at[j]) for j in range(3)]
+        word_win = [keep.tile([P, T], U16, name="word_win%d" % z, align_bytes=256) for z in range(PASSES)]
+        raw = [keep.tile([P, PASSES, PACK * Q], F32, name="raw%d" % j, align_bytes=256) for j in range(1)]
 
         def load_words(z):
             nc.scalar.dma_start(out=word_win[z][:].bitcast(I32), in_=voc_words[z].bitcast(I32))
 
-        def load_hidden(j):
-            nc.scalar.dma_start(out=raw[j][:], in_=hidden[j].rearrange("(z p t) q -> p z (t q)", z=PASSES, t=PACK))
+        def load_hidden(j, queue):
+            queue.dma_start(out=raw[j][:], in_=hidden[j].rearrange("(z p t) q -> p z (t q)", z=PASSES, t=PACK))
 
         load_words(0)
-        load_hidden(0)
+        load_hidden(0, nc.scalar)
         load_words(1)
-        load_hidden(1)
 
         warm = keep.tile([P, 1], F32, name="warm")
+        warm_out = keep.tile([P, 1], F32, name="warm_out")
         nc.gpsimd.memset(warm[:], 0.0)
 
         plane = [keep.tile([P, I], U8, name="plane%d" % z, align_bytes=64) for z in range(PASSES)]
         for z in range(PASSES):
             nc.vector.memset(plane[z][:].bitcast(I32), 0)
 
-        scale_g = stage.tile([P, I], U8, name="scale_g", offset=2 * raw_bytes + 128)
+        scale_g = keep.tile([P, I], U8, name="scale_g", align_bytes=64)
         nc.vector.tensor_copy(out=scale_g[:], in_=scale_win[:].indirect(offsets[:]))
         for z in range(PASSES):
             for quad in range(4):
@@ -80,14 +79,20 @@ def tile_attend_mixsoftmax_kernel(tc, ha, hb, hc, voc_words, voc_scales, pia, pi
                     out=plane[z][32 * quad : 32 * quad + 4, :].bitcast(I32),
                     in_=scale_g[row : row + 4, :].bitcast(I32),
                 )
+                if (z, quad) == (1, 1):
+                    raw.append(stage.tile([P, PASSES, PACK * Q], F32, name="raw1", offset=0))
+                    load_hidden(1, nc.sync)
 
-        share = [stage.tile([P, 1], F32, name="share%d" % j, offset=2 * raw_bytes + 128 + 64 * j) for j in range(3)]
+        raw.append(stage.tile([P, PASSES, PACK * Q], F32, name="raw2", offset=4352))
+        load_hidden(2, nc.sync)
+        share = [stage.tile([P, 1], F32, name="share%d" % j, offset=4096 + 64 * j) for j in range(3)]
         for j in range(3):
             nc.sync.dma_start(out=share[j][:], in_=shares[j])
 
         codes = [keep.tile([P, PASSES * Q], U32, name="codes%d" % j, align_bytes=64) for j in range(3)]
         hscale = [keep.tile([P, PASSES * Q], U8, name="hscale%d" % j, align_bytes=64) for j in range(3)]
-        grouped = [keep.tile([P, PASSES * Q * PACK], BF16, name="grouped%d" % j, tag="hold%d" % j, align_bytes=64) for j in range(3)]
+        grouped = [keep.tile([P, PASSES * Q * PACK], BF16, name="grouped%d" % j, tag="hold%d" % j, align_bytes=64) for j in range(2)]
+        grouped.append(late.tile([P, PASSES * Q * PACK], BF16, name="grouped2", offset=0, align_bytes=64))
 
         def cast(j):
             for z in range(PASSES):
@@ -102,8 +107,6 @@ def tile_attend_mixsoftmax_kernel(tc, ha, hb, hc, voc_words, voc_scales, pia, pi
         first = keep.tile([P, I], U16, name="first", align_bytes=64)
         nc.vector.tensor_copy(out=first[:], in_=word_win[0][:].indirect(offsets[:]))
         cast(0)
-        load_hidden(2)
-        warm_out = stage.tile([P, 1], F32, name="warm_out", offset=64)
         nc.scalar.activation(out=warm_out[:], in_=warm[:], func=ACT.Exp)
         quantise(0)
         second = keep.tile([P, I], U16, name="second", tag="hold0", align_bytes=64)
@@ -117,9 +120,8 @@ def tile_attend_mixsoftmax_kernel(tc, ha, hb, hc, voc_words, voc_scales, pia, pi
             return (first, second)[z][:, h * HALF : (h + 1) * HALF]
 
         bank = [[psum.tile([P, HALF], F32, name="bank%d_%d" % (j, h)) for h in range(HALVES)] for j in range(3)]
-        quantise(1)
-        quantise(2)
-        for j in range(3):
+
+        def score(j):
             for h in range(HALVES):
                 for z in range(PASSES):
                     nc.tensor.matmul_mx(
@@ -132,57 +134,87 @@ def tile_attend_mixsoftmax_kernel(tc, ha, hb, hc, voc_words, voc_scales, pia, pi
                         stop=(z == PASSES - 1),
                     )
 
-        prob = [stage.tile([P, I], F32, name="prob0", offset=raw_at[2])]
+        prob = [stage.tile([P, I], F32, name="prob0", offset=4352)]
         prob += [keep.tile([P, I], F32, name="prob%d" % j) for j in (1, 2)]
-        negated = [keep.tile([P, I], F32, name="negated%d" % j) for j in range(3)]
-        total = [keep.tile([P, 1], F32, name="total_%d" % j) for j in range(3)]
-        coef = [keep.tile([P, 1], F32, name="coef_%d" % j) for j in range(3)]
+        sums = [keep.tile([P, HALVES], F32, name="sums%d" % j) for j in range(3)]
+        rescale = [keep.tile([P, HALVES], F32, name="rescale%d" % j) for j in range(3)]
+        terms = [keep.tile([P, HALVES], F32, name="terms%d" % j) for j in range(3)]
+        total = [keep.tile([P, 1], F32, name="total%d" % j) for j in range(3)]
+        inv = [keep.tile([P, 1], F32, name="inv%d" % j) for j in range(3)]
+        coef = [keep.tile([P, HALVES], F32, name="coef%d" % j) for j in range(3)]
         mix = [keep.tile([P, I], F32, name="mix%d" % j) for j in range(3)]
-        part, inv = {}, {}
+        low, lowest = {}, {}
 
-        def first_max(j):
-            part[j] = keep.tile([P, 1], F32, name="part%d" % j, tag=("part0", "hold2", "part2")[j], align_bytes=64)
-            nc.vector.tensor_scalar(
-                out=negated[j][:, 0:HALF], in0=bank[j][0][:], scalar1=-1.0, scalar2=None,
-                op0=ALU.mult, op1=ALU.min, accum_out=part[j][:],
+        def half_max(j, h):
+            nc.vector.tensor_reduce(out=low[j][:, h : h + 1], in_=bank[j][h][:], axis=AX.X, op=ALU.max, negate=True)
+            nc.scalar.activation(
+                out=prob[j][:, h * HALF : (h + 1) * HALF], in_=bank[j][h][:], func=ACT.Exp,
+                bias=low[j][:, h : h + 1], scale=1.0, accum_out=sums[j][:, h : h + 1],
             )
 
-        def second_max(j):
-            low = keep.tile([P, 1], F32, name="low%d" % j, tag=("hold1", "low1", "low2")[j], align_bytes=64)
-            nc.vector.tensor_scalar(
-                out=negated[j][:, HALF:I], in0=bank[j][1][:], scalar1=-1.0, scalar2=part[j][:],
-                op0=ALU.mult, op1=ALU.min, accum_out=low[:],
+        def row_max(j):
+            nc.vector.tensor_reduce(out=lowest[j][:], in_=low[j][:], axis=AX.X, op=ALU.min)
+            nc.scalar.activation(out=rescale[j][:], in_=low[j][:], func=ACT.Exp, bias=lowest[j][:], scale=-1.0)
+
+        def row_sum(j):
+            nc.vector.scalar_tensor_tensor(
+                out=terms[j][:], in0=sums[j][:], scalar=1.0 / OUT_SCALE, in1=rescale[j][:],
+                op0=ALU.mult, op1=ALU.mult, accum_out=total[j][:],
             )
-            nc.scalar.activation(out=prob[j][:], in_=negated[j][:], func=ACT.Exp, bias=low[:], scale=-1.0, accum_out=total[j][:])
 
         def invert(j):
-            inv[j] = keep.tile([P, 1], F32, name="inv%d" % j, tag=("hold2", "part2", "inv2")[j], align_bytes=64)
             nc.vector.reciprocal(out=inv[j][:], in_=total[j][:])
 
         def weight(j):
-            nc.vector.tensor_scalar(out=coef[j][:], in0=inv[j][:], scalar1=share[j][:], scalar2=OUT_SCALE, op0=ALU.mult, op1=ALU.mult)
+            nc.vector.tensor_scalar(out=coef[j][:], in0=rescale[j][:], scalar1=inv[j][:], scalar2=share[j][:], op0=ALU.mult, op1=ALU.mult)
+
+        def first_term(h):
+            cs = slice(h * HALF, (h + 1) * HALF)
+            if h == 0:
+                nc.vector.tensor_scalar(out=mix[0][:, cs], in0=prob[0][:, cs], scalar1=coef[0][:, h : h + 1], scalar2=None, op0=ALU.mult)
+            else:
+                nc.scalar.activation(out=mix[0][:, cs], in_=prob[0][:, cs], func=ACT.Copy, scale=coef[0][:, h : h + 1])
 
         def add_term(j, c0, c1):
+            h = c0 // HALF
             nc.vector.scalar_tensor_tensor(
-                out=mix[j][:, c0:c1], in0=prob[j][:, c0:c1], scalar=coef[j][:], in1=mix[j - 1][:, c0:c1],
+                out=mix[j][:, c0:c1], in0=prob[j][:, c0:c1], scalar=coef[j][:, h : h + 1], in1=mix[j - 1][:, c0:c1],
                 op0=ALU.mult, op1=ALU.add,
             )
 
-        first_max(0)
-        second_max(0)
-        first_max(1)
-        second_max(1)
+        quantise(1)
+        score(0)
+        score(1)
+        low[0] = keep.tile([P, HALVES], F32, name="low0", tag="hold1", align_bytes=64)
+        half_max(0, 0)
+        half_max(0, 1)
+        quantise(2)
+        score(2)
+        lowest[0] = late.tile([P, 1], F32, name="lowest0", offset=0, align_bytes=64)
+        low[1] = late.tile([P, HALVES], F32, name="low1", offset=64, align_bytes=64)
+        low[2] = keep.tile([P, HALVES], F32, name="low2")
+        lowest[1] = keep.tile([P, 1], F32, name="lowest1")
+        lowest[2] = keep.tile([P, 1], F32, name="lowest2")
+        row_max(0)
+        half_max(1, 0)
+        half_max(1, 1)
+        row_max(1)
+        row_sum(0)
+        half_max(2, 0)
         invert(0)
-        first_max(2)
+        half_max(2, 1)
         weight(0)
-        second_max(2)
-        invert(1)
-        nc.vector.tensor_scalar(out=mix[0][:], in0=prob[0][:], scalar1=coef[0][:], scalar2=None, op0=ALU.mult)
-        weight(1)
+        row_max(2)
+        row_sum(2)
         invert(2)
         weight(2)
-        add_term(1, 0, HALF)
-        add_term(1, HALF, I)
-        for c0 in range(0, I, STORE):
-            add_term(2, c0, c0 + STORE)
-            nc.sync.dma_start(out=out[:, c0 : c0 + STORE], in_=mix[2][:, c0 : c0 + STORE])
+        row_sum(1)
+        invert(1)
+        weight(1)
+        first_term(0)
+        first_term(1)
+        for h in range(HALVES):
+            add_term(1, h * HALF, (h + 1) * HALF)
+            for c0 in range(h * HALF, (h + 1) * HALF, STORE):
+                add_term(2, c0, c0 + STORE)
+                nc.sync.dma_start(out=out[:, c0 : c0 + STORE], in_=mix[2][:, c0 : c0 + STORE])

from contextlib import ExitStack

import concourse.mybir as mybir

F32 = mybir.dt.float32
BF16 = mybir.dt.bfloat16
I32 = mybir.dt.int32
U32 = mybir.dt.uint32
U16 = mybir.dt.uint16
U8 = mybir.dt.uint8
FP8X4 = mybir.dt.float8_e4m3fn_x4
FP4X4 = mybir.dt.float4_e2m1fn_x4
ALU = mybir.AluOpType
ACT = mybir.ActivationFunctionType
AX = mybir.AxisListType

D, T, I, Q = 1024, 4096, 1024, 128
P = 128
PACK = 4
PASSES = D // (P * PACK)
HALF = 512
HALVES = I // HALF
LIST_COLS = I // 16
SCALE_ROWS = 16
SCALE_BASE = P - PASSES * SCALE_ROWS
OUT_SCALE = 512.0
STORE = 256

FLOPS = 3 * 2 * D * Q * I


def tile_attend_mixsoftmax_kernel(tc, ha, hb, hc, voc_words, voc_scales, pia, pib, pic, offs, out):
    nc = tc.nc
    hidden = (ha, hb, hc)
    shares = (pia, pib, pic)
    with ExitStack() as ctx:
        keep = ctx.enter_context(tc.tile_pool(name="keep", bufs=1))
        stage = ctx.enter_context(tc.tile_pool(name="stage", bufs=1))
        late = ctx.enter_context(tc.tile_pool(name="late", bufs=1))
        psum = ctx.enter_context(tc.psum_pool(name="psum", bufs=1))

        offsets = keep.tile([P, LIST_COLS], U16, name="offsets")
        nc.sync.dma_start(offsets[:], offs)

        scale_win = stage.tile([P, T], U8, name="scale_win", offset=3840)
        nc.scalar.dma_start(
            out=scale_win[SCALE_BASE:P, :].bitcast(I32),
            in_=voc_scales.rearrange("z f t -> (z f) t").bitcast(I32),
        )
        nc.vector.memset(scale_win[0:SCALE_BASE, :].bitcast(I32), 0)

        word_win = [keep.tile([P, T], U16, name="word_win%d" % z, align_bytes=256) for z in range(PASSES)]
        raw = [keep.tile([P, PASSES, PACK * Q], F32, name="raw%d" % j, align_bytes=256) for j in range(1)]

        def load_words(z):
            nc.scalar.dma_start(out=word_win[z][:].bitcast(I32), in_=voc_words[z].bitcast(I32))

        def load_hidden(j, queue):
            queue.dma_start(out=raw[j][:], in_=hidden[j].rearrange("(z p t) q -> p z (t q)", z=PASSES, t=PACK))

        load_words(0)
        load_hidden(0, nc.scalar)
        load_words(1)

        warm = keep.tile([P, 1], F32, name="warm")
        warm_out = keep.tile([P, 1], F32, name="warm_out")
        nc.gpsimd.memset(warm[:], 0.0)

        plane = [keep.tile([P, I], U8, name="plane%d" % z, align_bytes=64) for z in range(PASSES)]
        for z in range(PASSES):
            nc.vector.memset(plane[z][:].bitcast(I32), 0)

        scale_g = keep.tile([P, I], U8, name="scale_g", align_bytes=64)
        nc.vector.tensor_copy(out=scale_g[:], in_=scale_win[:].indirect(offsets[:]))
        for z in range(PASSES):
            for quad in range(4):
                row = SCALE_BASE + SCALE_ROWS * z + 4 * quad
                nc.sync.dma_start(
                    out=plane[z][32 * quad : 32 * quad + 4, :].bitcast(I32),
                    in_=scale_g[row : row + 4, :].bitcast(I32),
                )
                if (z, quad) == (1, 1):
                    raw.append(stage.tile([P, PASSES, PACK * Q], F32, name="raw1", offset=0))
                    load_hidden(1, nc.sync)

        raw.append(stage.tile([P, PASSES, PACK * Q], F32, name="raw2", offset=4352))
        load_hidden(2, nc.sync)
        share = [stage.tile([P, 1], F32, name="share%d" % j, offset=4096 + 64 * j) for j in range(3)]
        for j in range(3):
            nc.sync.dma_start(out=share[j][:], in_=shares[j])

        codes = [keep.tile([P, PASSES * Q], U32, name="codes%d" % j, align_bytes=64) for j in range(3)]
        hscale = [keep.tile([P, PASSES * Q], U8, name="hscale%d" % j, align_bytes=64) for j in range(3)]
        grouped = [keep.tile([P, PASSES * Q * PACK], BF16, name="grouped%d" % j, tag="hold%d" % j, align_bytes=64) for j in range(2)]
        grouped.append(late.tile([P, PASSES * Q * PACK], BF16, name="grouped2", offset=0, align_bytes=64))

        def cast(j):
            for z in range(PASSES):
                nc.scalar.copy(
                    out=grouped[j][:, z * Q * PACK : (z + 1) * Q * PACK].rearrange("p (c i t) -> p c t i", i=4, t=PACK),
                    in_=raw[j][:, z, :].rearrange("p (t c i) -> p c t i", i=4, t=PACK),
                )

        def quantise(j):
            nc.vector.quantize_mx(out=codes[j][:].bitcast(FP8X4), scales=hscale[j][:], in_=grouped[j][:])

        first = keep.tile([P, I], U16, name="first", align_bytes=64)
        nc.vector.tensor_copy(out=first[:], in_=word_win[0][:].indirect(offsets[:]))
        cast(0)
        nc.scalar.activation(out=warm_out[:], in_=warm[:], func=ACT.Exp)
        quantise(0)
        second = keep.tile([P, I], U16, name="second", tag="hold0", align_bytes=64)
        cols = LIST_COLS // HALVES
        for h in range(HALVES):
            nc.vector.tensor_copy(out=second[:, h * HALF : (h + 1) * HALF], in_=word_win[1][:].indirect(offsets[:, h * cols : (h + 1) * cols]))
        cast(1)
        cast(2)

        def words(z, h):
            return (first, second)[z][:, h * HALF : (h + 1) * HALF]

        bank = [[psum.tile([P, HALF], F32, name="bank%d_%d" % (j, h)) for h in range(HALVES)] for j in range(3)]

        def score(j):
            for h in range(HALVES):
                for z in range(PASSES):
                    nc.tensor.matmul_mx(
                        out=bank[j][h][:],
                        lhsT=codes[j][:, z * Q : (z + 1) * Q].bitcast(FP8X4),
                        lhsT_scale=hscale[j][:, z * Q : (z + 1) * Q],
                        rhs=words(z, h).bitcast(FP4X4),
                        rhs_scale=plane[z][:, h * HALF : (h + 1) * HALF],
                        start=(z == 0),
                        stop=(z == PASSES - 1),
                    )

        prob = [stage.tile([P, I], F32, name="prob0", offset=4352)]
        prob += [keep.tile([P, I], F32, name="prob%d" % j) for j in (1, 2)]
        sums = [keep.tile([P, HALVES], F32, name="sums%d" % j) for j in range(3)]
        rescale = [keep.tile([P, HALVES], F32, name="rescale%d" % j) for j in range(3)]
        terms = [keep.tile([P, HALVES], F32, name="terms%d" % j) for j in range(3)]
        total = [keep.tile([P, 1], F32, name="total%d" % j) for j in range(3)]
        inv = [keep.tile([P, 1], F32, name="inv%d" % j) for j in range(3)]
        coef = [keep.tile([P, HALVES], F32, name="coef%d" % j) for j in range(3)]
        mix = [keep.tile([P, I], F32, name="mix%d" % j) for j in range(3)]
        low, lowest = {}, {}

        def half_max(j, h):
            nc.vector.tensor_reduce(out=low[j][:, h : h + 1], in_=bank[j][h][:], axis=AX.X, op=ALU.max, negate=True)
            nc.scalar.activation(
                out=prob[j][:, h * HALF : (h + 1) * HALF], in_=bank[j][h][:], func=ACT.Exp,
                bias=low[j][:, h : h + 1], scale=1.0, accum_out=sums[j][:, h : h + 1],
            )

        def row_max(j):
            nc.vector.tensor_reduce(out=lowest[j][:], in_=low[j][:], axis=AX.X, op=ALU.min)
            nc.scalar.activation(out=rescale[j][:], in_=low[j][:], func=ACT.Exp, bias=lowest[j][:], scale=-1.0)

        def row_sum(j):
            nc.vector.scalar_tensor_tensor(
                out=terms[j][:], in0=sums[j][:], scalar=1.0 / OUT_SCALE, in1=rescale[j][:],
                op0=ALU.mult, op1=ALU.mult, accum_out=total[j][:],
            )

        def invert(j):
            nc.vector.reciprocal(out=inv[j][:], in_=total[j][:])

        def weight(j):
            nc.vector.tensor_scalar(out=coef[j][:], in0=rescale[j][:], scalar1=inv[j][:], scalar2=share[j][:], op0=ALU.mult, op1=ALU.mult)

        def first_term(h):
            cs = slice(h * HALF, (h + 1) * HALF)
            if h == 0:
                nc.vector.tensor_scalar(out=mix[0][:, cs], in0=prob[0][:, cs], scalar1=coef[0][:, h : h + 1], scalar2=None, op0=ALU.mult)
            else:
                nc.scalar.activation(out=mix[0][:, cs], in_=prob[0][:, cs], func=ACT.Copy, scale=coef[0][:, h : h + 1])

        def add_term(j, c0, c1):
            h = c0 // HALF
            nc.vector.scalar_tensor_tensor(
                out=mix[j][:, c0:c1], in0=prob[j][:, c0:c1], scalar=coef[j][:, h : h + 1], in1=mix[j - 1][:, c0:c1],
                op0=ALU.mult, op1=ALU.add,
            )

        quantise(1)
        score(0)
        score(1)
        low[0] = keep.tile([P, HALVES], F32, name="low0", tag="hold1", align_bytes=64)
        half_max(0, 0)
        half_max(0, 1)
        quantise(2)
        score(2)
        lowest[0] = late.tile([P, 1], F32, name="lowest0", offset=0, align_bytes=64)
        low[1] = late.tile([P, HALVES], F32, name="low1", offset=64, align_bytes=64)
        low[2] = keep.tile([P, HALVES], F32, name="low2")
        lowest[1] = keep.tile([P, 1], F32, name="lowest1")
        lowest[2] = keep.tile([P, 1], F32, name="lowest2")
        row_max(0)
        half_max(1, 0)
        half_max(1, 1)
        row_max(1)
        row_sum(0)
        half_max(2, 0)
        invert(0)
        half_max(2, 1)
        weight(0)
        row_max(2)
        row_sum(2)
        invert(2)
        weight(2)
        row_sum(1)
        invert(1)
        weight(1)
        first_term(0)
        first_term(1)
        for h in range(HALVES):
            add_term(1, h * HALF, (h + 1) * HALF)
            for c0 in range(h * HALF, (h + 1) * HALF, STORE):
                add_term(2, c0, c0 + STORE)
                nc.sync.dma_start(out=out[:, c0 : c0 + STORE], in_=mix[2][:, c0 : c0 + STORE])
